import numpy as np
import ml_dtypes


def mxq(x, axis, fmt="e4m3"):
    dtype, down = {"e4m3": (ml_dtypes.float8_e4m3fn, 7), "e5m2": (ml_dtypes.float8_e5m2, 14)}[fmt]
    v = np.moveaxis(np.asarray(x, np.float32).astype(ml_dtypes.bfloat16).astype(np.float64), axis, -1)
    blocks = v.reshape(v.shape[:-1] + (-1, 32))
    amax = np.abs(blocks).max(-1, keepdims=True)
    byte = np.maximum(np.where(amax > 0, np.frexp(amax)[1] - 1 + 127, 0) - down, 1)
    scale = np.exp2(byte - 127.0)
    codes = (blocks / scale).astype(np.float32).astype(dtype).astype(np.float64)
    return np.moveaxis((codes * scale).reshape(v.shape), -1, axis)


WIDE = False


def mx_kscale(k):
    if not WIDE:
        return np.ones(k)
    levels = np.array([10, -10, 5, -5, 0])
    if k % 512:
        return np.exp2(np.random.permutation(np.resize(levels, k // 32))).repeat(32)
    a = np.empty((k // 512, 16))
    for p in range(k // 512):
        a[p, :8] = np.random.permutation(np.resize(levels, 8))
        for g in range(8):
            far = levels[np.abs(levels - a[p, g]) >= 10]
            a[p, g + 8] = far[np.random.randint(len(far))]
    return np.exp2(a.ravel()).repeat(32)


def f64(x):
    return np.asarray(x).astype(np.float64)


def striped(idx):
    return np.tile(idx.reshape(-1, 16).T, (8, 1)).astype(np.uint16)


def unstriped(offs):
    return offs[:16].T.reshape(-1).astype(np.int64)


def pack_weight(w):
    k, n = w.shape
    w = f64(np.asarray(w, np.float32).astype(ml_dtypes.bfloat16)).reshape(k // 32, 32, n)
    amax = np.abs(w).max(1)
    byte = np.clip(np.where(amax > 0, np.frexp(amax)[1] - 1 + 127 - 7, 1), 1, 254)
    scaled = (w * np.exp2(127.0 - byte)[:, None, :]).reshape(k, n).astype(np.float32)
    words = np.ascontiguousarray(scaled.reshape(k // 512, 128, 4, n).transpose(0, 1, 3, 2)).astype(ml_dtypes.float8_e4m3fn).view(np.uint8)
    return words, np.ascontiguousarray(byte.astype(np.uint8).reshape(k // 512, 16, n))


def unpack_weight(words, scales):
    g, p, n, _ = words.shape
    vals = np.ascontiguousarray(words).view(ml_dtypes.float8_e4m3fn).astype(np.float64) * np.repeat(np.exp2(scales.astype(np.float64) - 127.0), 8, axis=1)[..., None]
    return vals.transpose(0, 1, 3, 2).reshape(g * 512, n)


K, T, S, V = 512, 2048, 512, 512
P = 2 ** 7


def setup_inputs():
    n = np.random.standard_normal
    s = mx_kscale(K)[:, None]
    packed_xT = pack_weight(n((K, T)) * s)
    packed_eT = pack_weight(n((K, T)) * s)
    return {
        "x_words": packed_xT[0],
        "x_scales": packed_xT[1],
        "hT": (n((K, V)) / np.sqrt(K) / s).astype(np.float32),
        "e_words": packed_eT[0],
        "e_scales": packed_eT[1],
        "lena": (np.tile(np.random.uniform(0.4, 2.0, T), (P, 1))).astype(np.float32),
        "lenb": (np.tile(np.random.uniform(0.4, 2.0, T), (P, 1))).astype(np.float32),
        "idf": (np.random.uniform(0.5, 4.0, (V, 1))).astype(np.float32),
        "offs": striped(np.random.permutation(T)[:S]),
    }


def reference(x_words, x_scales, hT, e_words, e_scales, lena, lenb, idf, offs):
    hTq = mxq(f64(hT), 0, "e4m3")
    xq = unpack_weight(x_words, x_scales)[:, unstriped(offs)]
    ya = hTq.T @ xq
    tfa = np.log(np.exp(ya) + 1.0)
    e_offs = unpack_weight(e_words, e_scales)[:, unstriped(offs)]
    yb = hTq.T @ e_offs
    tfb = np.log(np.exp(yb) + 1.0)
    tf = 2.2 * (tfa / (0.6 * (f64(lena)[:1][:, unstriped(offs)]) + 0.4)) + tfb / (0.75 * (f64(lenb)[:1][:, unstriped(offs)]) + 0.25)
    return f64(idf) * (((tf + 1.0) / (0.5 * tf + 3.0)) * np.log(tf + 1.0))

@@ -1,0 +1,185 @@
+from contextlib import ExitStack
+
+import concourse.mybir as mybir
+from concourse.masks import make_identity
+
+F32 = mybir.dt.float32
+BF16 = mybir.dt.bfloat16
+I32 = mybir.dt.int32
+U32 = mybir.dt.uint32
+U16 = mybir.dt.uint16
+U8 = mybir.dt.uint8
+FP8X4 = mybir.dt.float8_e4m3fn_x4
+ALU = mybir.AluOpType
+ACT = mybir.ActivationFunctionType
+
+P = 128
+K = 512
+T = 2048
+S = 512
+V = 512
+TILES = 4
+HALF = 256
+FLOOR_AT = 30.0
+LN_5 = 1.6094379124341003
+
+FLOPS = 2 * 2 * K * S * V
+
+
+def tile_picked_ybm25f_log_p_kernel(
+    tc, x_words, x_scales, hT, e_words, e_scales, lena, lenb, idf, offs, out
+):
+    nc = tc.nc
+    with ExitStack() as ctx:
+        held = ctx.enter_context(tc.tile_pool(name="held", bufs=1))
+        psum = ctx.enter_context(tc.psum_pool(name="psum", bufs=1))
+
+        offsets = held.tile([P, S // 16], U16, name="offsets")
+        nc.sync.dma_start(offsets[:], offs)
+
+        h_raw = held.tile([P, 4, V], F32, name="h_raw", tag="h_raw")
+        nc.sync.dma_start(h_raw[:], hT.rearrange("(p j) n -> p j n", j=4))
+
+        def load_words(name, table):
+            window = held.tile([P, T], U32, name=name, tag=name)
+            nc.sync.dma_start(window[:].bitcast(I32), table[0].rearrange("p n t -> p (n t)").bitcast(I32))
+            return window
+
+        words = [load_words("x_window", x_words)]
+
+        ident = held.tile([P, P], F32, name="ident")
+        make_identity(nc, ident[:])
+
+        planes = []
+        for name, engine in (("x", nc.vector), ("e", nc.gpsimd)):
+            plane = held.tile([P, T], U8, name=name + "_plane")
+            engine.memset(plane[:].bitcast(I32), 0)
+            planes.append(plane)
+        zero = held.tile([P, 1], F32, name="zero", tag="e_window")
+        nc.vector.memset(zero[:], 0.0)
+        lens = held.tile([P, T], F32, name="lens")
+        nc.vector.memset(lens[:], 0.0)
+
+        for f, table in enumerate((x_scales, e_scales)):
+            for q in range(4):
+                queue = nc.scalar if f == 0 else nc.gpsimd
+                queue.dma_start(
+                    planes[f][32 * q : 32 * q + 4, :].bitcast(I32), table[0, 4 * q : 4 * q + 4, :].bitcast(I32)
+                )
+        floor = held.tile([P, 1], F32, name="floor")
+        nc.scalar.activation(floor[:], zero[:], ACT.Sigmoid, bias=-FLOOR_AT)
+        nc.scalar.dma_start(lens[0:1, :], lena[0:1, :])
+        nc.scalar.dma_start(lens[1:2, :], lenb[0:1, :])
+        words.append(load_words("e_window", e_words))
+
+        def gather_scales(f):
+            picked = held.tile([P, S], U8, name="picked_scales%d" % f, align_bytes=64)
+            nc.vector.tensor_copy(picked[:], planes[f][:].indirect(offsets[:]))
+            return picked
+
+        def gather_words(f, half):
+            picked = held.tile([P, HALF], U32, name="picked_words%d_%d" % (f, half), align_bytes=64)
+            nc.vector.tensor_copy(picked[:], words[f][:].indirect(offsets[:, 16 * half : 16 * (half + 1)]))
+            return picked
+
+        scales = [gather_scales(0)]
+
+        picked_lens = held.tile([P, S], F32, name="picked_lens")
+        nc.vector.tensor_copy(picked_lens[:], lens[:].indirect(offsets[:]))
+        lens_t = psum.tile([P, TILES, P], F32, name="lens_t", tag="bank7")
+        for j in range(TILES):
+            nc.tensor.transpose(lens_t[:, j, :], picked_lens[:, j * P : (j + 1) * P], ident[:])
+        norm = held.tile([P, 2, TILES], F32, name="norm")
+        nc.vector.tensor_scalar(norm[:, 0, :], lens_t[:, :, 0], 0.6 / 2.2, 0.4 / 2.2, ALU.mult, ALU.add)
+        nc.vector.tensor_scalar(norm[:, 1, :], lens_t[:, :, 1], 0.75, 0.25, ALU.mult, ALU.add)
+        weight = held.tile([P, 2, TILES], F32, name="weight")
+        nc.vector.reciprocal(weight[:], norm[:])
+        neg_weight = held.tile([P, 2, TILES], F32, name="neg_weight")
+        nc.vector.tensor_scalar_mul(neg_weight[:], weight[:], -1.0)
+
+        h_bf = held.tile([P, V, 4], BF16, name="h_bf", align_bytes=64)
+        h_words = held.tile([P, V], U32, name="h_words", align_bytes=64)
+        h_scales = held.tile([P, V], U8, name="h_scales", align_bytes=64)
+        for half in range(2):
+            cols = slice(half * HALF, (half + 1) * HALF)
+            nc.scalar.copy(
+                h_bf[:, cols, :].rearrange("p (c i) t -> p c t i", i=4),
+                h_raw[:, :, cols].rearrange("p t (c i) -> p c t i", i=4),
+            )
+            nc.vector.quantize_mx(
+                out=h_words[:, cols].bitcast(FP8X4),
+                scales=h_scales[:, cols],
+                in_=h_bf[:, cols, :].rearrange("p n t -> p (n t)"),
+            )
+
+        idf_cols = held.tile([P, TILES], F32, name="idf_cols", tag="h_raw")
+        with nc.allow_non_contiguous_dma(reason="one value a term"):
+            nc.sync.dma_start(idf_cols[:], idf.rearrange("(m p) o -> p (m o)", p=P))
+
+        sig = [held.tile([P, 2, V], F32, name="sig%d" % j) for j in range(TILES)]
+        scaled = [held.tile([P, 2, V], F32, name="scaled%d" % j) for j in range(TILES)]
+        scores = {}
+        for f in range(2):
+            if f == 1:
+                scales.append(gather_scales(1))
+            for half in range(2):
+                picked = gather_words(f, half)
+                for i in range(2):
+                    j = 2 * half + i
+                    y = psum.tile([P, V], F32, name="y%d_%d" % (f, j), tag="bank%d" % (4 * f + j))
+                    nc.tensor.matmul_mx(
+                        out=y[:],
+                        lhsT=picked[:, i * P : (i + 1) * P].bitcast(FP8X4),
+                        lhsT_scale=scales[f][:, j * P : (j + 1) * P],
+                        rhs=h_words[:].bitcast(FP8X4),
+                        rhs_scale=h_scales[:],
+                        start=True,
+                        stop=True,
+                    )
+                    nc.scalar.activation(sig[j][:, f, :], y[:], ACT.Sigmoid, scale=-1.0)
+                    scores[(f, j)] = y
+        for f in range(2):
+            for j in range(TILES):
+                nc.vector.tensor_scalar_mul(scaled[j][:, f, :], scores[(f, j)][:], weight[:, f, j : j + 1])
+        idf2 = held.tile([P, TILES], F32, name="idf2")
+        nc.vector.tensor_scalar_mul(idf2[:], idf_cols[:], 2.0)
+
+        logs = held.tile([P, 2, TILES, 2, HALF], F32, name="logs", tag="e_window")
+        counts = held.tile([P, 2, TILES, 2, HALF], F32, name="counts", tag="counts")
+        tf = [psum.tile([P, S], F32, name="tf%d" % m, tag="bank%d" % m) for m in range(TILES)]
+        for half in range(2):
+            cols = slice(half * HALF, (half + 1) * HALF)
+            for j in range(TILES):
+                nc.scalar.activation(logs[:, half, j, :, :], sig[j][:, :, cols], ACT.Ln, bias=floor[:])
+                for f in range(2):
+                    nc.vector.scalar_tensor_tensor(
+                        counts[:, half, j, f, :],
+                        logs[:, half, j, f, :],
+                        neg_weight[:, f, j : j + 1],
+                        scaled[j][:, f, cols],
+                        ALU.mult,
+                        ALU.max,
+                    )
+                for i in range(2):
+                    for f in range(2):
+                        nc.tensor.matmul(
+                            tf[2 * half + i][:, j * P : (j + 1) * P],
+                            counts[:, half, j, f, i * P : (i + 1) * P],
+                            ident[:],
+                            is_transpose=True,
+                            start=(f == 0),
+                            stop=(f == 1),
+                        )
+        log_u = held.tile([P, TILES, S], F32, name="log_u")
+        for m in range(TILES):
+            nc.scalar.activation(log_u[:, m, :], tf[m][:], ACT.Ln, bias=1.0)
+
+        ratio = held.tile([P, TILES, S], F32, name="ratio", tag="counts")
+        result = held.tile([P, TILES, S], F32, name="result")
+        pieces = [(m, 0, S) for m in range(TILES - 1)] + [(TILES - 1, 0, HALF), (TILES - 1, HALF, S)]
+        for m, lo, hi in pieces:
+            nc.scalar.activation(ratio[:, m, lo:hi], log_u[:, m, lo:hi], ACT.Sigmoid, bias=-LN_5)
+            nc.vector.scalar_tensor_tensor(
+                result[:, m, lo:hi], ratio[:, m, lo:hi], idf2[:, m : m + 1], log_u[:, m, lo:hi], ALU.mult, ALU.mult
+            )
+            nc.sync.dma_start(out[m * P : (m + 1) * P, lo:hi], result[:, m, lo:hi])

@@ -20,6 +20,7 @@ S = 512
 V = 512
 TILES = 4
 HALF = 256
+SCALE_ROW = (0, 4)
 FLOOR_AT = 30.0
 LN_5 = 1.6094379124341003
 
@@ -37,40 +38,41 @@ def tile_picked_ybm25f_log_p_kernel(
         offsets = held.tile([P, S // 16], U16, name="offsets")
         nc.sync.dma_start(offsets[:], offs)
 
-        h_raw = held.tile([P, 4, V], F32, name="h_raw", tag="h_raw")
+        h_raw = held.tile([P, 4, V], F32, name="h_raw")
         nc.sync.dma_start(h_raw[:], hT.rearrange("(p j) n -> p j n", j=4))
 
-        def load_words(name, table):
-            window = held.tile([P, T], U32, name=name, tag=name)
+        def load_words(tag, table):
+            window = held.tile([P, T], U32, name="window_" + tag, tag=tag)
             nc.sync.dma_start(window[:].bitcast(I32), table[0].rearrange("p n t -> p (n t)").bitcast(I32))
             return window
 
-        words = [load_words("x_window", x_words)]
+        def load_scales(tag, table, row):
+            plane = held.tile([P, T], U8, name="plane_" + tag, tag=tag)
+            nc.vector.memset(plane[:].bitcast(I32), 0)
+            for q in range(4):
+                nc.sync.dma_start(
+                    plane[32 * q + row : 32 * q + row + 4, :].bitcast(I32), table[0, 4 * q : 4 * q + 4, :].bitcast(I32)
+                )
+            return plane
 
         ident = held.tile([P, P], F32, name="ident")
         make_identity(nc, ident[:])
 
-        planes = []
-        for name, engine in (("x", nc.vector), ("e", nc.gpsimd)):
-            plane = held.tile([P, T], U8, name=name + "_plane")
-            engine.memset(plane[:].bitcast(I32), 0)
-            planes.append(plane)
-        zero = held.tile([P, 1], F32, name="zero", tag="e_window")
-        nc.vector.memset(zero[:], 0.0)
+        planes = [load_scales("x_plane", x_scales, SCALE_ROW[0])]
+        floor_at = held.tile([P, 1], F32, name="floor_at")
+        nc.vector.memset(floor_at[:], -FLOOR_AT)
+        floor = held.tile([P, 1], F32, name="floor")
+        nc.scalar.activation(floor[:], floor_at[:], ACT.Sigmoid)
         lens = held.tile([P, T], F32, name="lens")
         nc.vector.memset(lens[:], 0.0)
-
-        for f, table in enumerate((x_scales, e_scales)):
-            for q in range(4):
-                queue = nc.scalar if f == 0 else nc.gpsimd
-                queue.dma_start(
-                    planes[f][32 * q : 32 * q + 4, :].bitcast(I32), table[0, 4 * q : 4 * q + 4, :].bitcast(I32)
-                )
-        floor = held.tile([P, 1], F32, name="floor")
-        nc.scalar.activation(floor[:], zero[:], ACT.Sigmoid, bias=-FLOOR_AT)
-        nc.scalar.dma_start(lens[0:1, :], lena[0:1, :])
-        nc.scalar.dma_start(lens[1:2, :], lenb[0:1, :])
+        nc.sync.dma_start(lens[8:9, :], lena[0:1, :])
+        nc.sync.dma_start(lens[12:13, :], lenb[0:1, :])
+        words = [load_words("x_window", x_words)]
+        planes.append(load_scales("e_plane", e_scales, SCALE_ROW[1]))
         words.append(load_words("e_window", e_words))
+        idf_cols = held.tile([P, TILES], F32, name="idf_cols")
+        with nc.allow_non_contiguous_dma(reason="one value a term"):
+            nc.sync.dma_start(idf_cols[:], idf.rearrange("(m p) o -> p (m o)", p=P))
 
         def gather_scales(f):
             picked = held.tile([P, S], U8, name="picked_scales%d" % f, align_bytes=64)
@@ -90,8 +92,8 @@ def tile_picked_ybm25f_log_p_kernel(
         for j in range(TILES):
             nc.tensor.transpose(lens_t[:, j, :], picked_lens[:, j * P : (j + 1) * P], ident[:])
         norm = held.tile([P, 2, TILES], F32, name="norm")
-        nc.vector.tensor_scalar(norm[:, 0, :], lens_t[:, :, 0], 0.6 / 2.2, 0.4 / 2.2, ALU.mult, ALU.add)
-        nc.vector.tensor_scalar(norm[:, 1, :], lens_t[:, :, 1], 0.75, 0.25, ALU.mult, ALU.add)
+        nc.vector.tensor_scalar(norm[:, 0, :], lens_t[:, :, 8], 0.6 / 2.2, 0.4 / 2.2, ALU.mult, ALU.add)
+        nc.vector.tensor_scalar(norm[:, 1, :], lens_t[:, :, 12], 0.75, 0.25, ALU.mult, ALU.add)
         weight = held.tile([P, 2, TILES], F32, name="weight")
         nc.vector.reciprocal(weight[:], norm[:])
         neg_weight = held.tile([P, 2, TILES], F32, name="neg_weight")
@@ -112,12 +114,7 @@ def tile_picked_ybm25f_log_p_kernel(
                 in_=h_bf[:, cols, :].rearrange("p n t -> p (n t)"),
             )
 
-        idf_cols = held.tile([P, TILES], F32, name="idf_cols", tag="h_raw")
-        with nc.allow_non_contiguous_dma(reason="one value a term"):
-            nc.sync.dma_start(idf_cols[:], idf.rearrange("(m p) o -> p (m o)", p=P))
-
         sig = [held.tile([P, 2, V], F32, name="sig%d" % j) for j in range(TILES)]
-        scaled = [held.tile([P, 2, V], F32, name="scaled%d" % j) for j in range(TILES)]
         scores = {}
         for f in range(2):
             if f == 1:
@@ -130,7 +127,7 @@ def tile_picked_ybm25f_log_p_kernel(
                     nc.tensor.matmul_mx(
                         out=y[:],
                         lhsT=picked[:, i * P : (i + 1) * P].bitcast(FP8X4),
-                        lhsT_scale=scales[f][:, j * P : (j + 1) * P],
+                        lhsT_scale=scales[f][SCALE_ROW[f] : P, j * P : (j + 1) * P],
                         rhs=h_words[:].bitcast(FP8X4),
                         rhs_scale=h_scales[:],
                         start=True,
@@ -138,13 +135,15 @@ def tile_picked_ybm25f_log_p_kernel(
                     )
                     nc.scalar.activation(sig[j][:, f, :], y[:], ACT.Sigmoid, scale=-1.0)
                     scores[(f, j)] = y
+        work = held.tile([P, 2, TILES * 2 * V], F32, name="work", tag="e_window")
+        scaled = work[:, 0, :].rearrange("p (j f n) -> p j f n", j=TILES, f=2)
+        logs = work[:, 1, :].rearrange("p (h j f n) -> p h j f n", h=2, j=TILES, f=2)
         for f in range(2):
             for j in range(TILES):
-                nc.vector.tensor_scalar_mul(scaled[j][:, f, :], scores[(f, j)][:], weight[:, f, j : j + 1])
+                nc.vector.tensor_scalar_mul(scaled[:, j, f, :], scores[(f, j)][:], weight[:, f, j : j + 1])
         idf2 = held.tile([P, TILES], F32, name="idf2")
         nc.vector.tensor_scalar_mul(idf2[:], idf_cols[:], 2.0)
 
-        logs = held.tile([P, 2, TILES, 2, HALF], F32, name="logs", tag="e_window")
         counts = held.tile([P, 2, TILES, 2, HALF], F32, name="counts", tag="counts")
         tf = [psum.tile([P, S], F32, name="tf%d" % m, tag="bank%d" % m) for m in range(TILES)]
         for half in range(2):
@@ -156,7 +155,7 @@ def tile_picked_ybm25f_log_p_kernel(
                         counts[:, half, j, f, :],
                         logs[:, half, j, f, :],
                         neg_weight[:, f, j : j + 1],
-                        scaled[j][:, f, cols],
+                        scaled[:, j, f, cols],
                         ALU.mult,
                         ALU.max,
                     )

@@ -38,7 +38,7 @@ def tile_picked_ybm25f_log_p_kernel(
         offsets = held.tile([P, S // 16], U16, name="offsets")
         nc.sync.dma_start(offsets[:], offs)
 
-        h_raw = held.tile([P, 4, V], F32, name="h_raw")
+        h_raw = held.tile([P, 4, V], F32, name="h_raw", tag="h_raw")
         nc.sync.dma_start(h_raw[:], hT.rearrange("(p j) n -> p j n", j=4))
 
         def load_words(tag, table):
@@ -46,8 +46,8 @@ def tile_picked_ybm25f_log_p_kernel(
             nc.sync.dma_start(window[:].bitcast(I32), table[0].rearrange("p n t -> p (n t)").bitcast(I32))
             return window
 
-        def load_scales(tag, table, row):
-            plane = held.tile([P, T], U8, name="plane_" + tag, tag=tag)
+        def load_scales(name, table, row):
+            plane = held.tile([P, T], U8, name=name)
             nc.vector.memset(plane[:].bitcast(I32), 0)
             for q in range(4):
                 nc.sync.dma_start(
@@ -55,24 +55,31 @@ def tile_picked_ybm25f_log_p_kernel(
                 )
             return plane
 
+        def constant(name, zero, value):
+            column = held.tile([P, 1], F32, name=name)
+            nc.vector.tensor_scalar_add(column[:], zero[:], value)
+            return column
+
         ident = held.tile([P, P], F32, name="ident")
         make_identity(nc, ident[:])
 
         planes = [load_scales("x_plane", x_scales, SCALE_ROW[0])]
-        floor_at = held.tile([P, 1], F32, name="floor_at")
-        nc.vector.memset(floor_at[:], -FLOOR_AT)
-        floor = held.tile([P, 1], F32, name="floor")
-        nc.scalar.activation(floor[:], floor_at[:], ACT.Sigmoid)
-        lens = held.tile([P, T], F32, name="lens")
+        zeros = []
+        for tag in ("x_window", "e_window"):
+            zero = held.tile([P, 1], F32, name="zero_" + tag, tag=tag)
+            nc.vector.memset(zero[:], 0.0)
+            zeros.append(zero)
+        lens = held.tile([P, T], F32, name="lens", tag="lens", align_bytes=64)
         nc.vector.memset(lens[:], 0.0)
         nc.sync.dma_start(lens[8:9, :], lena[0:1, :])
         nc.sync.dma_start(lens[12:13, :], lenb[0:1, :])
+        floor_at = constant("floor_at", zeros[0], -FLOOR_AT)
         words = [load_words("x_window", x_words)]
         planes.append(load_scales("e_plane", e_scales, SCALE_ROW[1]))
+        neg_ln5 = constant("neg_ln5", zeros[1], -LN_5)
         words.append(load_words("e_window", e_words))
-        idf_cols = held.tile([P, TILES], F32, name="idf_cols")
-        with nc.allow_non_contiguous_dma(reason="one value a term"):
-            nc.sync.dma_start(idf_cols[:], idf.rearrange("(m p) o -> p (m o)", p=P))
+        floor = held.tile([P, 1], F32, name="floor")
+        nc.scalar.activation(floor[:], floor_at[:], ACT.Sigmoid)
 
         def gather_scales(f):
             picked = held.tile([P, S], U8, name="picked_scales%d" % f, align_bytes=64)
@@ -91,34 +98,32 @@ def tile_picked_ybm25f_log_p_kernel(
         lens_t = psum.tile([P, TILES, P], F32, name="lens_t", tag="bank7")
         for j in range(TILES):
             nc.tensor.transpose(lens_t[:, j, :], picked_lens[:, j * P : (j + 1) * P], ident[:])
-        norm = held.tile([P, 2, TILES], F32, name="norm")
-        nc.vector.tensor_scalar(norm[:, 0, :], lens_t[:, :, 8], 0.6 / 2.2, 0.4 / 2.2, ALU.mult, ALU.add)
-        nc.vector.tensor_scalar(norm[:, 1, :], lens_t[:, :, 12], 0.75, 0.25, ALU.mult, ALU.add)
-        weight = held.tile([P, 2, TILES], F32, name="weight")
-        nc.vector.reciprocal(weight[:], norm[:])
-        neg_weight = held.tile([P, 2, TILES], F32, name="neg_weight")
-        nc.vector.tensor_scalar_mul(neg_weight[:], weight[:], -1.0)
 
         h_bf = held.tile([P, V, 4], BF16, name="h_bf", align_bytes=64)
-        h_words = held.tile([P, V], U32, name="h_words", align_bytes=64)
+        h_words = held.tile([P, V], U32, name="h_words", tag="lens", align_bytes=64)
         h_scales = held.tile([P, V], U8, name="h_scales", align_bytes=64)
-        for half in range(2):
-            cols = slice(half * HALF, (half + 1) * HALF)
-            nc.scalar.copy(
-                h_bf[:, cols, :].rearrange("p (c i) t -> p c t i", i=4),
-                h_raw[:, :, cols].rearrange("p t (c i) -> p c t i", i=4),
-            )
-            nc.vector.quantize_mx(
-                out=h_words[:, cols].bitcast(FP8X4),
-                scales=h_scales[:, cols],
-                in_=h_bf[:, cols, :].rearrange("p n t -> p (n t)"),
-            )
+        nc.scalar.copy(
+            h_bf[:].rearrange("p (c i) t -> p c t i", i=4), h_raw[:].rearrange("p t (c i) -> p c t i", i=4)
+        )
+        nc.vector.quantize_mx(
+            out=h_words[:].bitcast(FP8X4), scales=h_scales[:], in_=h_bf[:].rearrange("p n t -> p (n t)")
+        )
+
+        idf_cols = held.tile([P, TILES], F32, name="idf_cols", tag="h_raw")
+        with nc.allow_non_contiguous_dma(reason="one value a term"):
+            nc.sync.dma_start(idf_cols[:], idf.rearrange("(m p) o -> p (m o)", p=P))
+
+        norm = held.tile([P, 2, TILES], F32, name="norm")
+        nc.scalar.activation(norm[:, 0, :], lens_t[:, :, 8], ACT.Identity, scale=-0.6 / 2.2, bias=-0.4 / 2.2)
+        nc.scalar.activation(norm[:, 1, :], lens_t[:, :, 12], ACT.Identity, scale=-0.75, bias=-0.25)
 
         sig = [held.tile([P, 2, V], F32, name="sig%d" % j) for j in range(TILES)]
         scores = {}
         for f in range(2):
             if f == 1:
                 scales.append(gather_scales(1))
+                neg_weight = held.tile([P, 2, TILES], F32, name="neg_weight", tag="x_window")
+                nc.vector.reciprocal(neg_weight[:], norm[:])
             for half in range(2):
                 picked = gather_words(f, half)
                 for i in range(2):
@@ -140,7 +145,9 @@ def tile_picked_ybm25f_log_p_kernel(
         logs = work[:, 1, :].rearrange("p (h j f n) -> p h j f n", h=2, j=TILES, f=2)
         for f in range(2):
             for j in range(TILES):
-                nc.vector.tensor_scalar_mul(scaled[:, j, f, :], scores[(f, j)][:], weight[:, f, j : j + 1])
+                nc.vector.tensor_scalar(
+                    scaled[:, j, f, :], scores[(f, j)][:], neg_weight[:, f, j : j + 1], -1.0, ALU.mult, ALU.mult
+                )
         idf2 = held.tile([P, TILES], F32, name="idf2")
         nc.vector.tensor_scalar_mul(idf2[:], idf_cols[:], 2.0)
 
@@ -175,10 +182,14 @@ def tile_picked_ybm25f_log_p_kernel(
 
         ratio = held.tile([P, TILES, S], F32, name="ratio", tag="counts")
         result = held.tile([P, TILES, S], F32, name="result")
-        pieces = [(m, 0, S) for m in range(TILES - 1)] + [(TILES - 1, 0, HALF), (TILES - 1, HALF, S)]
-        for m, lo, hi in pieces:
-            nc.scalar.activation(ratio[:, m, lo:hi], log_u[:, m, lo:hi], ACT.Sigmoid, bias=-LN_5)
-            nc.vector.scalar_tensor_tensor(
-                result[:, m, lo:hi], ratio[:, m, lo:hi], idf2[:, m : m + 1], log_u[:, m, lo:hi], ALU.mult, ALU.mult
-            )
-            nc.sync.dma_start(out[m * P : (m + 1) * P, lo:hi], result[:, m, lo:hi])
+        for m in range(TILES):
+            for half in range(2):
+                cols = slice(half * HALF, (half + 1) * HALF)
+                nc.scalar.activation(ratio[:, m, cols], log_u[:, m, cols], ACT.Sigmoid, bias=neg_ln5[:])
+                nc.vector.scalar_tensor_tensor(
+                    result[:, m, cols], ratio[:, m, cols], idf2[:, m : m + 1], log_u[:, m, cols], ALU.mult, ALU.mult
+                )
+                if m == TILES - 1:
+                    nc.sync.dma_start(out[m * P : (m + 1) * P, cols], result[:, m, cols])
+            if m < TILES - 1:
+                nc.sync.dma_start(out[m * P : (m + 1) * P, :], result[:, m, :])

@@ -20,6 +20,8 @@ S = 512
 V = 512
 TILES = 4
 HALF = 256
+SCALAR_TERMS = 352
+TERM_PARTS = ((0, 2), (2, 3), (3, 4))
 SCALE_ROW = (0, 4)
 FLOOR_AT = 30.0
 LN_5 = 1.6094379124341003
@@ -37,9 +39,6 @@ def tile_picked_ybm25f_log_p_kernel(
 
         offsets = held.tile([P, S // 16], U16, name="offsets")
         nc.sync.dma_start(offsets[:], offs)
-
-        h_raw = held.tile([P, 4, V], F32, name="h_raw", tag="h_raw")
-        nc.sync.dma_start(h_raw[:], hT.rearrange("(p j) n -> p j n", j=4))
 
         def load_words(tag, table):
             window = held.tile([P, T], U32, name="window_" + tag, tag=tag)
@@ -60,30 +59,32 @@ def tile_picked_ybm25f_log_p_kernel(
             nc.vector.tensor_scalar_add(column[:], zero[:], value)
             return column
 
-        ident = held.tile([P, P], F32, name="ident")
-        make_identity(nc, ident[:])
-
-        planes = [load_scales("x_plane", x_scales, SCALE_ROW[0])]
         zeros = []
-        for tag in ("x_window", "e_window"):
+        for tag in ("h_raw", "x_window", "e_window"):
             zero = held.tile([P, 1], F32, name="zero_" + tag, tag=tag)
             nc.vector.memset(zero[:], 0.0)
             zeros.append(zero)
+        planes = [load_scales("x_plane", x_scales, SCALE_ROW[0])]
+        one = constant("one", zeros[0], 1.0)
+        h_raw = held.tile([P, 4, V], F32, name="h_raw", tag="h_raw")
+        nc.sync.dma_start(h_raw[:], hT.rearrange("(p j) n -> p j n", j=4))
+        ident = held.tile([P, P], F32, name="ident")
+        make_identity(nc, ident[:])
         lens = held.tile([P, T], F32, name="lens", tag="lens", align_bytes=64)
         nc.vector.memset(lens[:], 0.0)
         nc.sync.dma_start(lens[8:9, :], lena[0:1, :])
         nc.sync.dma_start(lens[12:13, :], lenb[0:1, :])
-        floor_at = constant("floor_at", zeros[0], -FLOOR_AT)
+        floor_at = constant("floor_at", zeros[1], -FLOOR_AT)
         words = [load_words("x_window", x_words)]
         planes.append(load_scales("e_plane", e_scales, SCALE_ROW[1]))
-        neg_ln5 = constant("neg_ln5", zeros[1], -LN_5)
+        neg_ln5 = constant("neg_ln5", zeros[2], -LN_5)
         words.append(load_words("e_window", e_words))
         floor = held.tile([P, 1], F32, name="floor")
         nc.scalar.activation(floor[:], floor_at[:], ACT.Sigmoid)
 
-        def gather_scales(f):
-            picked = held.tile([P, S], U8, name="picked_scales%d" % f, align_bytes=64)
-            nc.vector.tensor_copy(picked[:], planes[f][:].indirect(offsets[:]))
+        def gather_scales(f, half):
+            picked = held.tile([P, HALF], U8, name="picked_scales%d_%d" % (f, half), align_bytes=64)
+            nc.vector.tensor_copy(picked[:], planes[f][:].indirect(offsets[:, 16 * half : 16 * (half + 1)]))
             return picked
 
         def gather_words(f, half):
@@ -91,7 +92,7 @@ def tile_picked_ybm25f_log_p_kernel(
             nc.vector.tensor_copy(picked[:], words[f][:].indirect(offsets[:, 16 * half : 16 * (half + 1)]))
             return picked
 
-        scales = [gather_scales(0)]
+        x_picked_scales = [gather_scales(0, half) for half in range(2)]
 
         picked_lens = held.tile([P, S], F32, name="picked_lens")
         nc.vector.tensor_copy(picked_lens[:], lens[:].indirect(offsets[:]))
@@ -102,9 +103,11 @@ def tile_picked_ybm25f_log_p_kernel(
         h_bf = held.tile([P, V, 4], BF16, name="h_bf", align_bytes=64)
         h_words = held.tile([P, V], U32, name="h_words", tag="lens", align_bytes=64)
         h_scales = held.tile([P, V], U8, name="h_scales", align_bytes=64)
-        nc.scalar.copy(
-            h_bf[:].rearrange("p (c i) t -> p c t i", i=4), h_raw[:].rearrange("p t (c i) -> p c t i", i=4)
-        )
+        for copy, cols in ((nc.scalar.copy, slice(0, SCALAR_TERMS)), (nc.vector.tensor_copy, slice(SCALAR_TERMS, V))):
+            copy(
+                h_bf[:, cols, :].rearrange("p (c i) t -> p c t i", i=4),
+                h_raw[:, :, cols].rearrange("p t (c i) -> p c t i", i=4),
+            )
         nc.vector.quantize_mx(
             out=h_words[:].bitcast(FP8X4), scales=h_scales[:], in_=h_bf[:].rearrange("p n t -> p (n t)")
         )
@@ -120,11 +123,8 @@ def tile_picked_ybm25f_log_p_kernel(
         sig = [held.tile([P, 2, V], F32, name="sig%d" % j) for j in range(TILES)]
         scores = {}
         for f in range(2):
-            if f == 1:
-                scales.append(gather_scales(1))
-                neg_weight = held.tile([P, 2, TILES], F32, name="neg_weight", tag="x_window")
-                nc.vector.reciprocal(neg_weight[:], norm[:])
             for half in range(2):
+                picked_scales = x_picked_scales[half] if f == 0 else gather_scales(1, half)
                 picked = gather_words(f, half)
                 for i in range(2):
                     j = 2 * half + i
@@ -132,7 +132,7 @@ def tile_picked_ybm25f_log_p_kernel(
                     nc.tensor.matmul_mx(
                         out=y[:],
                         lhsT=picked[:, i * P : (i + 1) * P].bitcast(FP8X4),
-                        lhsT_scale=scales[f][SCALE_ROW[f] : P, j * P : (j + 1) * P],
+                        lhsT_scale=picked_scales[SCALE_ROW[f] : P, i * P : (i + 1) * P],
                         rhs=h_words[:].bitcast(FP8X4),
                         rhs_scale=h_scales[:],
                         start=True,
@@ -140,9 +140,11 @@ def tile_picked_ybm25f_log_p_kernel(
                     )
                     nc.scalar.activation(sig[j][:, f, :], y[:], ACT.Sigmoid, scale=-1.0)
                     scores[(f, j)] = y
-        work = held.tile([P, 2, TILES * 2 * V], F32, name="work", tag="e_window")
-        scaled = work[:, 0, :].rearrange("p (j f n) -> p j f n", j=TILES, f=2)
-        logs = work[:, 1, :].rearrange("p (h j f n) -> p h j f n", h=2, j=TILES, f=2)
+        work = held.tile([P, 2 * TILES * (2 * V + 1)], F32, name="work", tag="e_window")
+        scaled = work[:, 0 : 2 * TILES * V].rearrange("p (j f n) -> p j f n", j=TILES, f=2)
+        logs = work[:, 2 * TILES * V : 4 * TILES * V].rearrange("p (j f n) -> p j f n", j=TILES, f=2)
+        neg_weight = work[:, 4 * TILES * V :].rearrange("p (f j) -> p f j", f=2)
+        nc.vector.reciprocal(neg_weight, norm[:])
         for f in range(2):
             for j in range(TILES):
                 nc.vector.tensor_scalar(
@@ -151,26 +153,26 @@ def tile_picked_ybm25f_log_p_kernel(
         idf2 = held.tile([P, TILES], F32, name="idf2")
         nc.vector.tensor_scalar_mul(idf2[:], idf_cols[:], 2.0)
 
-        counts = held.tile([P, 2, TILES, 2, HALF], F32, name="counts", tag="counts")
+        counts = held.tile([P, TILES, 2, V], F32, name="counts", tag="counts")
         tf = [psum.tile([P, S], F32, name="tf%d" % m, tag="bank%d" % m) for m in range(TILES)]
-        for half in range(2):
-            cols = slice(half * HALF, (half + 1) * HALF)
+        for first, last in TERM_PARTS:
+            cols = slice(first * P, last * P)
             for j in range(TILES):
-                nc.scalar.activation(logs[:, half, j, :, :], sig[j][:, :, cols], ACT.Ln, bias=floor[:])
+                nc.scalar.activation(logs[:, j, :, cols], sig[j][:, :, cols], ACT.Ln, bias=floor[:])
                 for f in range(2):
                     nc.vector.scalar_tensor_tensor(
-                        counts[:, half, j, f, :],
-                        logs[:, half, j, f, :],
+                        counts[:, j, f, cols],
+                        logs[:, j, f, cols],
                         neg_weight[:, f, j : j + 1],
                         scaled[:, j, f, cols],
                         ALU.mult,
                         ALU.max,
                     )
-                for i in range(2):
+                for m in range(first, last):
                     for f in range(2):
                         nc.tensor.matmul(
-                            tf[2 * half + i][:, j * P : (j + 1) * P],
-                            counts[:, half, j, f, i * P : (i + 1) * P],
+                            tf[m][:, j * P : (j + 1) * P],
+                            counts[:, j, f, m * P : (m + 1) * P],
                             ident[:],
                             is_transpose=True,
                             start=(f == 0),
@@ -178,7 +180,7 @@ def tile_picked_ybm25f_log_p_kernel(
                         )
         log_u = held.tile([P, TILES, S], F32, name="log_u")
         for m in range(TILES):
-            nc.scalar.activation(log_u[:, m, :], tf[m][:], ACT.Ln, bias=1.0)
+            nc.scalar.activation(log_u[:, m, :], tf[m][:], ACT.Ln, bias=one[:])
 
         ratio = held.tile([P, TILES, S], F32, name="ratio", tag="counts")
         result = held.tile([P, TILES, S], F32, name="result")

from contextlib import ExitStack

import concourse.mybir as mybir
from concourse.masks import make_identity

F32 = mybir.dt.float32
BF16 = mybir.dt.bfloat16
I32 = mybir.dt.int32
U32 = mybir.dt.uint32
U16 = mybir.dt.uint16
U8 = mybir.dt.uint8
FP8X4 = mybir.dt.float8_e4m3fn_x4
ALU = mybir.AluOpType
ACT = mybir.ActivationFunctionType

P = 128
K = 512
T = 2048
S = 512
V = 512
TILES = 4
HALF = 256
SCALAR_TERMS = 352
TERM_PARTS = ((0, 2), (2, 3), (3, 4))
SCALE_ROW = (0, 4)
FLOOR_AT = 30.0
LN_5 = 1.6094379124341003

FLOPS = 2 * 2 * K * S * V


def tile_picked_ybm25f_log_p_kernel(
    tc, x_words, x_scales, hT, e_words, e_scales, lena, lenb, idf, offs, out
):
    nc = tc.nc
    with ExitStack() as ctx:
        held = ctx.enter_context(tc.tile_pool(name="held", bufs=1))
        psum = ctx.enter_context(tc.psum_pool(name="psum", bufs=1))

        offsets = held.tile([P, S // 16], U16, name="offsets")
        nc.sync.dma_start(offsets[:], offs)

        def load_words(tag, table):
            window = held.tile([P, T], U32, name="window_" + tag, tag=tag)
            nc.sync.dma_start(window[:].bitcast(I32), table[0].rearrange("p n t -> p (n t)").bitcast(I32))
            return window

        def load_scales(name, table, row):
            plane = held.tile([P, T], U8, name=name)
            nc.vector.memset(plane[:].bitcast(I32), 0)
            for q in range(4):
                nc.sync.dma_start(
                    plane[32 * q + row : 32 * q + row + 4, :].bitcast(I32), table[0, 4 * q : 4 * q + 4, :].bitcast(I32)
                )
            return plane

        def constant(name, zero, value):
            column = held.tile([P, 1], F32, name=name)
            nc.vector.tensor_scalar_add(column[:], zero[:], value)
            return column

        zeros = []
        for tag in ("h_raw", "x_window", "e_window"):
            zero = held.tile([P, 1], F32, name="zero_" + tag, tag=tag)
            nc.vector.memset(zero[:], 0.0)
            zeros.append(zero)
        planes = [load_scales("x_plane", x_scales, SCALE_ROW[0])]
        one = constant("one", zeros[0], 1.0)
        h_raw = held.tile([P, 4, V], F32, name="h_raw", tag="h_raw")
        nc.sync.dma_start(h_raw[:], hT.rearrange("(p j) n -> p j n", j=4))
        ident = held.tile([P, P], F32, name="ident")
        make_identity(nc, ident[:])
        lens = held.tile([P, T], F32, name="lens", tag="lens", align_bytes=64)
        nc.vector.memset(lens[:], 0.0)
        nc.sync.dma_start(lens[8:9, :], lena[0:1, :])
        nc.sync.dma_start(lens[12:13, :], lenb[0:1, :])
        floor_at = constant("floor_at", zeros[1], -FLOOR_AT)
        words = [load_words("x_window", x_words)]
        planes.append(load_scales("e_plane", e_scales, SCALE_ROW[1]))
        neg_ln5 = constant("neg_ln5", zeros[2], -LN_5)
        words.append(load_words("e_window", e_words))
        floor = held.tile([P, 1], F32, name="floor")
        nc.scalar.activation(floor[:], floor_at[:], ACT.Sigmoid)

        def gather_scales(f, half):
            picked = held.tile([P, HALF], U8, name="picked_scales%d_%d" % (f, half), align_bytes=64)
            nc.vector.tensor_copy(picked[:], planes[f][:].indirect(offsets[:, 16 * half : 16 * (half + 1)]))
            return picked

        def gather_words(f, half):
            picked = held.tile([P, HALF], U32, name="picked_words%d_%d" % (f, half), align_bytes=64)
            nc.vector.tensor_copy(picked[:], words[f][:].indirect(offsets[:, 16 * half : 16 * (half + 1)]))
            return picked

        x_picked_scales = [gather_scales(0, half) for half in range(2)]

        picked_lens = held.tile([P, S], F32, name="picked_lens")
        nc.vector.tensor_copy(picked_lens[:], lens[:].indirect(offsets[:]))
        lens_t = psum.tile([P, TILES, P], F32, name="lens_t", tag="bank7")
        for j in range(TILES):
            nc.tensor.transpose(lens_t[:, j, :], picked_lens[:, j * P : (j + 1) * P], ident[:])

        h_bf = held.tile([P, V, 4], BF16, name="h_bf", align_bytes=64)
        h_words = held.tile([P, V], U32, name="h_words", tag="lens", align_bytes=64)
        h_scales = held.tile([P, V], U8, name="h_scales", align_bytes=64)
        for copy, cols in ((nc.scalar.copy, slice(0, SCALAR_TERMS)), (nc.vector.tensor_copy, slice(SCALAR_TERMS, V))):
            copy(
                h_bf[:, cols, :].rearrange("p (c i) t -> p c t i", i=4),
                h_raw[:, :, cols].rearrange("p t (c i) -> p c t i", i=4),
            )
        nc.vector.quantize_mx(
            out=h_words[:].bitcast(FP8X4), scales=h_scales[:], in_=h_bf[:].rearrange("p n t -> p (n t)")
        )

        idf_cols = held.tile([P, TILES], F32, name="idf_cols", tag="h_raw")
        with nc.allow_non_contiguous_dma(reason="one value a term"):
            nc.sync.dma_start(idf_cols[:], idf.rearrange("(m p) o -> p (m o)", p=P))

        norm = held.tile([P, 2, TILES], F32, name="norm")
        nc.scalar.activation(norm[:, 0, :], lens_t[:, :, 8], ACT.Identity, scale=-0.6 / 2.2, bias=-0.4 / 2.2)
        nc.scalar.activation(norm[:, 1, :], lens_t[:, :, 12], ACT.Identity, scale=-0.75, bias=-0.25)

        sig = [held.tile([P, 2, V], F32, name="sig%d" % j) for j in range(TILES)]
        scores = {}
        for f in range(2):
            for half in range(2):
                picked_scales = x_picked_scales[half] if f == 0 else gather_scales(1, half)
                picked = gather_words(f, half)
                for i in range(2):
                    j = 2 * half + i
                    y = psum.tile([P, V], F32, name="y%d_%d" % (f, j), tag="bank%d" % (4 * f + j))
                    nc.tensor.matmul_mx(
                        out=y[:],
                        lhsT=picked[:, i * P : (i + 1) * P].bitcast(FP8X4),
                        lhsT_scale=picked_scales[SCALE_ROW[f] : P, i * P : (i + 1) * P],
                        rhs=h_words[:].bitcast(FP8X4),
                        rhs_scale=h_scales[:],
                        start=True,
                        stop=True,
                    )
                    nc.scalar.activation(sig[j][:, f, :], y[:], ACT.Sigmoid, scale=-1.0)
                    scores[(f, j)] = y
        work = held.tile([P, 2 * TILES * (2 * V + 1)], F32, name="work", tag="e_window")
        scaled = work[:, 0 : 2 * TILES * V].rearrange("p (j f n) -> p j f n", j=TILES, f=2)
        logs = work[:, 2 * TILES * V : 4 * TILES * V].rearrange("p (j f n) -> p j f n", j=TILES, f=2)
        neg_weight = work[:, 4 * TILES * V :].rearrange("p (f j) -> p f j", f=2)
        nc.vector.reciprocal(neg_weight, norm[:])
        for f in range(2):
            for j in range(TILES):
                nc.vector.tensor_scalar(
                    scaled[:, j, f, :], scores[(f, j)][:], neg_weight[:, f, j : j + 1], -1.0, ALU.mult, ALU.mult
                )
        idf2 = held.tile([P, TILES], F32, name="idf2")
        nc.vector.tensor_scalar_mul(idf2[:], idf_cols[:], 2.0)

        counts = held.tile([P, TILES, 2, V], F32, name="counts", tag="counts")
        tf = [psum.tile([P, S], F32, name="tf%d" % m, tag="bank%d" % m) for m in range(TILES)]
        for first, last in TERM_PARTS:
            cols = slice(first * P, last * P)
            for j in range(TILES):
                nc.scalar.activation(logs[:, j, :, cols], sig[j][:, :, cols], ACT.Ln, bias=floor[:])
                for f in range(2):
                    nc.vector.scalar_tensor_tensor(
                        counts[:, j, f, cols],
                        logs[:, j, f, cols],
                        neg_weight[:, f, j : j + 1],
                        scaled[:, j, f, cols],
                        ALU.mult,
                        ALU.max,
                    )
                for m in range(first, last):
                    for f in range(2):
                        nc.tensor.matmul(
                            tf[m][:, j * P : (j + 1) * P],
                            counts[:, j, f, m * P : (m + 1) * P],
                            ident[:],
                            is_transpose=True,
                            start=(f == 0),
                            stop=(f == 1),
                        )
        log_u = held.tile([P, TILES, S], F32, name="log_u")
        for m in range(TILES):
            nc.scalar.activation(log_u[:, m, :], tf[m][:], ACT.Ln, bias=one[:])

        ratio = held.tile([P, TILES, S], F32, name="ratio", tag="counts")
        result = held.tile([P, TILES, S], F32, name="result")
        for m in range(TILES):
            for half in range(2):
                cols = slice(half * HALF, (half + 1) * HALF)
                nc.scalar.activation(ratio[:, m, cols], log_u[:, m, cols], ACT.Sigmoid, bias=neg_ln5[:])
                nc.vector.scalar_tensor_tensor(
                    result[:, m, cols], ratio[:, m, cols], idf2[:, m : m + 1], log_u[:, m, cols], ALU.mult, ALU.mult
                )
                if m == TILES - 1:
                    nc.sync.dma_start(out[m * P : (m + 1) * P, cols], result[:, m, cols])
            if m < TILES - 1:
                nc.sync.dma_start(out[m * P : (m + 1) * P, :], result[:, m, :])
